import numpy as np
CORES = [2,3,0,1]
N = 4
def setup_inputs(rng):
    return {"x": rng.standard_normal((N, 128, 512), dtype=np.float32)}
def reference(x):
    s = x.sum(axis=0, dtype=np.float64).astype(x.dtype)
    return {"y": np.broadcast_to(s, (N,) + s.shape)}

@@ -1,0 +1,56 @@
+from concourse.bass import DstId, RemoteDMATransfer
+from concourse.mybir import AluOpType
+
+B = 128
+
+SCRATCH = {
+    "xs": ("sbuf", [128, 512], "float32"),
+    "land": ("sbuf", [128, 512], "float32"),
+    "res": ("sbuf", [128, 512], "float32"),
+}
+SEMAPHORES = ["loaded", "seeded", "summed", "stored", "sent", "arrived", "gathered"]
+
+
+def rank_program(g, core, T, topo):
+    r = T.rank_of(core)
+    if r is None:
+        return
+    n = len(T.cores)
+    others = [j for j in range(n) if j != r]
+    a, b, c = others
+
+    def blk(t, j):
+        return t[:, j * B:(j + 1) * B]
+
+    def dst_id(j):
+        rid, pid, _se = topo.addr(T.cores[j])
+        return DstId(rid=rid, pnc=pid)
+
+    g.dma_start(T.xs[:], T.x[:]).then_inc(T.sem.loaded, 16)
+    g.dma_start(blk(T.res, r), blk(T.x, r)).then_inc(T.sem.seeded, 16)
+    g.wait_ge(T.sem.loaded, 16)
+
+    g.remote_dma_fused(
+        [RemoteDMATransfer(dst_ids=[dst_id(j)], dma_engine_mask=0xF << (4 * k), remote_sem=T.sem.arrived,
+                           src=blk(T.xs, j), dst=blk(T.land, r))
+         for k, j in enumerate(others)],
+        local_sem=T.sem.sent)
+    g.wait_ge(T.sem.arrived, 12)
+    g.wait_ge(T.sem.seeded, 16)
+
+    g.dma_start(blk(T.res, r), blk(T.land, a), accum_op=AluOpType.add).then_inc(T.sem.summed, 16)
+    g.dma_start(blk(T.land, b), blk(T.land, c), accum_op=AluOpType.add).then_inc(T.sem.summed, 16)
+    g.wait_ge(T.sem.summed, 32)
+
+    g.remote_dma_fused(
+        [RemoteDMATransfer(dst_ids=[dst_id(j) for j in others], dma_engine_mask=0xFFFF, remote_sem=T.sem.gathered,
+                           srcs=[blk(T.xs, r), blk(T.land, a), blk(T.land, b)],
+                           dsts=[blk(T.res, r) for _j in others], alu_op=1)],
+        local_sem=T.sem.sent)
+    g.dma_start(blk(T.res, r), blk(T.land, b), accum_op=AluOpType.add).then_inc(T.sem.summed, 16)
+    g.wait_ge(T.sem.summed, 48)
+    g.wait_ge(T.sem.gathered, 48)
+
+    g.dma_start(T.y[:], T.res[:]).then_inc(T.sem.stored, 16)
+    g.wait_ge(T.sem.stored, 16)
+    g.wait_ge(T.sem.sent, 28)

@@ -1,56 +1,42 @@
 from concourse.bass import DstId, RemoteDMATransfer
-from concourse.mybir import AluOpType
-
-B = 128
 
 SCRATCH = {
-    "xs": ("sbuf", [128, 512], "float32"),
-    "land": ("sbuf", [128, 512], "float32"),
-    "res": ("sbuf", [128, 512], "float32"),
+    "xs": ("dram", [4, 128, 128], "float32"),
+    "land": ("dram", [4, 128, 128], "float32"),
+    "res": ("dram", [4, 128, 128], "float32"),
 }
-SEMAPHORES = ["loaded", "seeded", "summed", "stored", "sent", "arrived", "gathered"]
+SEMAPHORES = ["loaded", "stored", "sent", "arrived", "gathered"]
+
+SIM_CORES = 8
 
 
 def rank_program(g, core, T, topo):
-    r = T.rank_of(core)
-    if r is None:
-        return
     n = len(T.cores)
-    others = [j for j in range(n) if j != r]
-    a, b, c = others
+    helpers = [c for c in range(SIM_CORES) if T.rank_of(c) is None][:n]
 
-    def blk(t, j):
-        return t[:, j * B:(j + 1) * B]
-
-    def dst_id(j):
-        rid, pid, _se = topo.addr(T.cores[j])
+    def dst_id(c):
+        rid, pid, _se = topo.addr(c)
         return DstId(rid=rid, pnc=pid)
 
-    g.dma_start(T.xs[:], T.x[:]).then_inc(T.sem.loaded, 16)
-    g.dma_start(blk(T.res, r), blk(T.x, r)).then_inc(T.sem.seeded, 16)
-    g.wait_ge(T.sem.loaded, 16)
-
-    g.remote_dma_fused(
-        [RemoteDMATransfer(dst_ids=[dst_id(j)], dma_engine_mask=0xF << (4 * k), remote_sem=T.sem.arrived,
-                           src=blk(T.xs, j), dst=blk(T.land, r))
-         for k, j in enumerate(others)],
-        local_sem=T.sem.sent)
-    g.wait_ge(T.sem.arrived, 12)
-    g.wait_ge(T.sem.seeded, 16)
-
-    g.dma_start(blk(T.res, r), blk(T.land, a), accum_op=AluOpType.add).then_inc(T.sem.summed, 16)
-    g.dma_start(blk(T.land, b), blk(T.land, c), accum_op=AluOpType.add).then_inc(T.sem.summed, 16)
-    g.wait_ge(T.sem.summed, 32)
-
-    g.remote_dma_fused(
-        [RemoteDMATransfer(dst_ids=[dst_id(j) for j in others], dma_engine_mask=0xFFFF, remote_sem=T.sem.gathered,
-                           srcs=[blk(T.xs, r), blk(T.land, a), blk(T.land, b)],
-                           dsts=[blk(T.res, r) for _j in others], alu_op=1)],
-        local_sem=T.sem.sent)
-    g.dma_start(blk(T.res, r), blk(T.land, b), accum_op=AluOpType.add).then_inc(T.sem.summed, 16)
-    g.wait_ge(T.sem.summed, 48)
-    g.wait_ge(T.sem.gathered, 48)
-
-    g.dma_start(T.y[:], T.res[:]).then_inc(T.sem.stored, 16)
-    g.wait_ge(T.sem.stored, 16)
-    g.wait_ge(T.sem.sent, 28)
+    r = T.rank_of(core)
+    if r is not None:
+        g.dma_start(T.xs[:], T.x[:]).then_inc(T.sem.loaded, 16)
+        g.wait_ge(T.sem.loaded, 16)
+        g.remote_dma_fused(
+            [RemoteDMATransfer(dst_ids=[dst_id(c)], dma_engine_mask=0xF << (4 * h), remote_sem=T.sem.arrived,
+                               src=T.xs[h], dst=T.land[r])
+             for h, c in enumerate(helpers)],
+            local_sem=T.sem.sent)
+        g.wait_ge(T.sem.gathered, 16 * n)
+        g.dma_start(T.y[:], T.res[:]).then_inc(T.sem.stored, 16)
+        g.wait_ge(T.sem.stored, 16)
+        g.wait_ge(T.sem.sent, 16)
+    elif core in helpers:
+        h = helpers.index(core)
+        g.wait_ge(T.sem.arrived, 4 * n)
+        g.remote_dma_fused(
+            [RemoteDMATransfer(dst_ids=[dst_id(c) for c in T.cores], dma_engine_mask=0xFFFF,
+                               remote_sem=T.sem.gathered,
+                               srcs=[T.land[j] for j in range(n)], dsts=[T.res[h] for _c in T.cores], alu_op=1)],
+            local_sem=T.sem.sent)
+        g.wait_ge(T.sem.sent, 16)

from concourse.bass import DstId, RemoteDMATransfer

SCRATCH = {
    "xs": ("dram", [4, 128, 128], "float32"),
    "land": ("dram", [4, 128, 128], "float32"),
    "res": ("dram", [4, 128, 128], "float32"),
}
SEMAPHORES = ["loaded", "stored", "sent", "arrived", "gathered"]

SIM_CORES = 8


def rank_program(g, core, T, topo):
    n = len(T.cores)
    helpers = [c for c in range(SIM_CORES) if T.rank_of(c) is None][:n]

    def dst_id(c):
        rid, pid, _se = topo.addr(c)
        return DstId(rid=rid, pnc=pid)

    r = T.rank_of(core)
    if r is not None:
        g.dma_start(T.xs[:], T.x[:]).then_inc(T.sem.loaded, 16)
        g.wait_ge(T.sem.loaded, 16)
        g.remote_dma_fused(
            [RemoteDMATransfer(dst_ids=[dst_id(c)], dma_engine_mask=0xF << (4 * h), remote_sem=T.sem.arrived,
                               src=T.xs[h], dst=T.land[r])
             for h, c in enumerate(helpers)],
            local_sem=T.sem.sent)
        g.wait_ge(T.sem.gathered, 16 * n)
        g.dma_start(T.y[:], T.res[:]).then_inc(T.sem.stored, 16)
        g.wait_ge(T.sem.stored, 16)
        g.wait_ge(T.sem.sent, 16)
    elif core in helpers:
        h = helpers.index(core)
        g.wait_ge(T.sem.arrived, 4 * n)
        g.remote_dma_fused(
            [RemoteDMATransfer(dst_ids=[dst_id(c) for c in T.cores], dma_engine_mask=0xFFFF,
                               remote_sem=T.sem.gathered,
                               srcs=[T.land[j] for j in range(n)], dsts=[T.res[h] for _c in T.cores], alu_op=1)],
            local_sem=T.sem.sent)
        g.wait_ge(T.sem.sent, 16)
